import numpy as np
import ml_dtypes


def mxq(x, axis, fmt="e4m3"):
    dtype, down = {"e4m3": (ml_dtypes.float8_e4m3fn, 7), "e5m2": (ml_dtypes.float8_e5m2, 14)}[fmt]
    v = np.moveaxis(np.asarray(x, np.float32).astype(ml_dtypes.bfloat16).astype(np.float64), axis, -1)
    blocks = v.reshape(v.shape[:-1] + (-1, 32))
    amax = np.abs(blocks).max(-1, keepdims=True)
    byte = np.maximum(np.where(amax > 0, np.frexp(amax)[1] - 1 + 127, 0) - down, 1)
    scale = np.exp2(byte - 127.0)
    codes = (blocks / scale).astype(np.float32).astype(dtype).astype(np.float64)
    return np.moveaxis((codes * scale).reshape(v.shape), -1, axis)


WIDE = False


def mx_kscale(k):
    if not WIDE:
        return np.ones(k)
    levels = np.array([10, -10, 5, -5, 0])
    if k % 512:
        return np.exp2(np.random.permutation(np.resize(levels, k // 32))).repeat(32)
    a = np.empty((k // 512, 16))
    for p in range(k // 512):
        a[p, :8] = np.random.permutation(np.resize(levels, 8))
        for g in range(8):
            far = levels[np.abs(levels - a[p, g]) >= 10]
            a[p, g + 8] = far[np.random.randint(len(far))]
    return np.exp2(a.ravel()).repeat(32)


def f64(x):
    return np.asarray(x).astype(np.float64)


def striped(idx):
    return np.tile(np.asarray(idx).reshape(-1, 16).T, (8, 1)).astype(np.uint16)


def unstriped(offs):
    return offs[:16].T.reshape(-1).astype(np.int64)


E2M1 = np.array([0.0, 0.5, 1.0, 1.5, 2.0, 3.0, 4.0, 6.0, -0.0, -0.5, -1.0, -1.5, -2.0, -3.0, -4.0, -6.0])


def pack_weight(w, fmt):
    k, n = w.shape
    w = f64(np.asarray(w, np.float32).astype(ml_dtypes.bfloat16)).reshape(k // 32, 32, n)
    amax = np.abs(w).max(1)
    if fmt == "e4m3":
        byte = np.frexp(amax)[1] - 1 + 127 - 7
    else:
        mant, ex = np.frexp(amax / 6.0)
        byte = np.where(mant > 0.5, ex, ex - 1) + 127
    byte = np.clip(np.where(amax > 0, byte, 1), 1, 254)
    scaled = (w * np.exp2(127.0 - byte)[:, None, :]).reshape(k, n).astype(np.float32)
    by_word = np.ascontiguousarray(scaled.reshape(k // 512, 128, 4, n).transpose(0, 1, 3, 2))
    if fmt == "e4m3":
        words = by_word.astype(ml_dtypes.float8_e4m3fn).view(np.uint8)
    else:
        c = by_word.astype(ml_dtypes.float4_e2m1fn).view(np.uint8) & 0xF
        words = (c[..., 0::2] | (c[..., 1::2] << 4)).reshape(k // 512, 128, 2 * n)
    return np.ascontiguousarray(words), np.ascontiguousarray(byte.astype(np.uint8).reshape(k // 512, 16, n))


def unpack_weight(words, scales, fmt):
    g, _, n = scales.shape
    words = np.ascontiguousarray(words).reshape(g, 128, n, -1)
    if fmt == "e4m3":
        vals = words.view(ml_dtypes.float8_e4m3fn).astype(np.float64)
    else:
        nib = np.empty((g, 128, n, 4), np.uint8)
        nib[..., 0::2] = words & 0xF
        nib[..., 1::2] = words >> 4
        vals = E2M1[nib]
    vals = vals * np.repeat(np.exp2(scales.astype(np.float64) - 127.0), 8, axis=1)[..., None]
    return vals.transpose(0, 1, 3, 2).reshape(g * 512, n)


def bf(x):
    return np.asarray(x, np.float32).astype(ml_dtypes.bfloat16)


def planes(Y):
    r, m = Y.shape
    b = f64(bf(Y)).reshape(r // 32, 32, m)
    amax = np.abs(b).max(1)
    byte = np.clip(np.where(amax > 0, np.frexp(amax)[1] - 1 + 127 - 7, 1), 1, 254)
    codes = (b * np.exp2(127.0 - byte)[:, None, :]).reshape(r, m).astype(np.float32).astype(ml_dtypes.float8_e4m3fn).view(np.uint8)
    words = codes.reshape(r // 512, 128, 4, m).transpose(0, 1, 3, 2)
    return np.ascontiguousarray(words), np.ascontiguousarray(byte.astype(np.uint8).reshape(r // 512, 16, m))


D, T, I, Q, E, N = 512, 2048, 512, 256, 512, 64


def setup_inputs():
    n = np.random.standard_normal
    idx = np.random.permutation(T)[:I]
    fd = mx_kscale(D)
    fi = mx_kscale(I)
    ti = np.ones(T)
    ti[idx] = fi
    keysp = pack_weight(n((D, T)) / fd[:, None], "e2m1")
    return {
        "query": (n((D, Q)) * 0.78 / np.sqrt(D) * fd[:, None]).astype(np.float32),
        "query2": (n((D, Q)) * 0.325 / np.sqrt(D) * fd[:, None]).astype(np.float32),
        "keys_words": keysp[0],
        "keys_scales": keysp[1],
        "lam": (np.random.uniform(0.8, 1.5, (Q, 1))).astype(np.float32),
        "sharp": (np.random.uniform(1.5, 3.0, (Q, 1))).astype(np.float32),
        "share": (np.random.uniform(0.5, 0.9, (Q, 1))).astype(np.float32),
        "os": (np.random.uniform(4.0, 16.0, (1, I)) * fi).astype(np.float32),
        "vals": (n((E, T)) / ti).astype(np.float32),
        "memq": (np.random.uniform(0.3, 1.0, (1, Q))).astype(np.float32),
        "offs": striped(idx),
    }


def reference(query, query2, keys_words, keys_scales, lam, sharp, share, os, vals, memq, offs):
    idx = unstriped(offs)
    keysu = unpack_weight(keys_words, keys_scales, "e2m1")
    queryq = mxq(f64(query), 0, "e4m3")
    keysidxg = keysu[:, idx]
    a = queryq.T @ keysidxg
    query2q = mxq(f64(query2), 0, "e4m3")
    b = query2q.T @ keysidxg
    bh0 = b.reshape(Q, N, I // N).max(axis=2)
    nb = b * (-1.0)
    bl0 = nb.reshape(Q, N, I // N).max(axis=2)
    bh1 = np.repeat(bh0, I // N, axis=1)
    bl1 = np.repeat(bl0, I // N, axis=1)
    s = np.maximum(np.minimum(a, bh1), bl1 * (-1.0)) * f64(lam)
    p = np.exp(s - np.max(s, axis=1, keepdims=True))
    r = p / np.sum(p, axis=1, keepdims=True)
    s2 = s * f64(sharp)
    p2 = np.exp(s2 - np.max(s2, axis=1, keepdims=True))
    r2 = p2 / np.sum(p2, axis=1, keepdims=True)
    w = r * f64(share) - r2 * (1.0 - f64(share))
    wo1 = w * f64(os)
    wt1 = wo1.T
    vt1 = f64(vals)[:, idx].T
    vt1q = mxq(vt1, 0, "e4m3")
    wt1q = mxq(wt1, 0, "e4m3")
    o = vt1q.T @ wt1q
    o1 = np.pad(o, ((0, 0), (1, 0)))[:, :Q]
    y = o - o1 * f64(memq)
    words, scales = planes(y)
    return y, words, scales

@@ -1,0 +1,296 @@
+from contextlib import ExitStack
+
+import concourse.mybir as mybir
+from concourse.masks import make_identity
+
+D, T, I, Q, E, PAGE = 512, 2048, 512, 256, 512, 8
+FLOPS = 2 * (2 * D * Q * I + I * E * Q)
+
+F32 = mybir.dt.float32
+BF16 = mybir.dt.bfloat16
+I32 = mybir.dt.int32
+U32 = mybir.dt.uint32
+U16 = mybir.dt.uint16
+U8 = mybir.dt.uint8
+FP8X4 = mybir.dt.float8_e4m3fn_x4
+FP4X4 = mybir.dt.float4_e2m1fn_x4
+ALU = mybir.AluOpType
+ACT = mybir.ActivationFunctionType
+AX = mybir.AxisListType
+
+P = 128
+PACK = 4
+QT = Q // P
+PAGES = I // PAGE
+
+
+def interleave_views(grouped, planes):
+    return (
+        grouped.rearrange("p (c i) t -> p c t i", i=4),
+        planes.rearrange("p t (c i) -> p c t i", i=4),
+    )
+
+
+def tile_attend_pagelimits_twoheats_rowchanges_pl_kernel(
+    tc, query, query2, keys_words, keys_scales, lam, sharp, share, slot_factor, vals, memq, offs, out_0, out_1, out_2
+):
+    nc = tc.nc
+    with ExitStack() as ctx:
+        sb = ctx.enter_context(tc.tile_pool(name="sb", bufs=1))
+        psum = ctx.enter_context(tc.psum_pool(name="psum", bufs=1))
+
+        offsets = sb.tile([P, I // 16], U16, name="offsets")
+        key_words = sb.tile([P, T], U16, name="key_words", tag="staged0")
+        key_scales = sb.tile([P, T], U8, name="key_scales", tag="staged1")
+        nc.vector.memset(key_scales[:].bitcast(I32), 0)
+        nc.sync.dma_start(offsets[:], offs)
+        nc.sync.dma_start(out=key_words[:].bitcast(I32), in_=keys_words[0].bitcast(I32))
+        q_raw = [
+            sb.tile([P, PACK, Q], F32, name="limit_query", tag="staged2"),
+        ]
+        nc.sync.dma_start(out=q_raw[0][:], in_=query2.rearrange("(p j) q -> p j q", j=PACK))
+        lam_c = sb.tile([P, QT], F32, name="lam_c", tag="staged3")
+        sharp_c = sb.tile([P, QT], F32, name="sharp_c")
+        share_c = sb.tile([P, QT], F32, name="share_c")
+        with nc.allow_non_contiguous_dma(reason="one value of each query row to its partition"):
+            for queue, col, src in ((nc.scalar, lam_c, lam), (nc.gpsimd, sharp_c, sharp), (nc.gpsimd, share_c, share)):
+                queue.dma_start(out=col[:], in_=src.rearrange("(c p) o -> p (c o)", p=P))
+        for quad in range(4):
+            nc.scalar.dma_start(
+                out=key_scales[32 * quad : 32 * quad + 4, :].bitcast(I32),
+                in_=keys_scales[0, 4 * quad : 4 * quad + 4, :].bitcast(I32),
+            )
+        os_c = sb.tile([P, PACK], F32, name="os_c")
+        nc.gpsimd.dma_start(out=os_c[:], in_=slot_factor.rearrange("o (s r) -> (o s) r", r=PACK))
+        mem_c = sb.tile([P, 2], F32, name="mem_c")
+        nc.gpsimd.dma_start(out=mem_c[:], in_=memq.rearrange("o (p t) -> (o p) t", t=2))
+        val_planes = vals.rearrange("(p t) n -> t p n", t=PACK)
+
+        neg_lam = sb.tile([P, QT], F32, name="neg_lam")
+        nc.vector.tensor_scalar(neg_lam[:], lam_c[:], -1.0, None, ALU.mult)
+        q_raw.append(sb.tile([P, PACK, Q], F32, name="score_query", tag="staged3"))
+        nc.sync.dma_start(out=q_raw[1][:], in_=query.rearrange("(p j) q -> p j q", j=PACK))
+        ident = sb.tile([P, P], F32, name="ident")
+        make_identity(nc, ident[:])
+        share_m1 = sb.tile([P, QT], F32, name="share_m1")
+        nc.gpsimd.tensor_scalar(share_m1[:], share_c[:], 1.0, -1.0, ALU.mult, ALU.add)
+
+        carried = sb.tile([P, PACK, Q], F32, name="carried")
+        nc.vector.memset(carried[:, :, 0:1], 0.0)
+
+        kg_words = sb.tile([P, I], U16, name="kg_words", align_bytes=64)
+        nc.vector.tensor_copy(kg_words[:], key_words[:].indirect(offsets[:]))
+        kg_scales = sb.tile([P, I], U8, name="kg_scales", align_bytes=64)
+        nc.vector.tensor_copy(kg_scales[:], key_scales[:].indirect(offsets[:]))
+
+        scores = []
+        for c in range(QT):
+            pair = []
+            for k, raw in enumerate(q_raw):
+                grouped = sb.tile([P, P, PACK], BF16, name="q_grouped", tag=("q_grouped0", "turn")[c], align_bytes=64)
+                dst, src = interleave_views(grouped[:], raw[:, :, c * P : (c + 1) * P])
+                nc.scalar.copy(dst, src)
+                codes = sb.tile([P, P], U32, name="q_codes%d%d" % (c, k), align_bytes=64)
+                scales = sb.tile([P, P], U8, name="q_scales%d%d" % (c, k), align_bytes=64)
+                nc.vector.quantize_mx(
+                    out=codes[:].bitcast(FP8X4), scales=scales[:], in_=grouped[:].rearrange("p w j -> p (w j)")
+                )
+                bank = psum.tile([P, I], F32, name="score%d%d" % (c, k), tag="bank%d" % (2 * c + k))
+                nc.tensor.matmul_mx(
+                    out=bank[:],
+                    lhsT=codes[:].bitcast(FP8X4),
+                    lhsT_scale=scales[:],
+                    rhs=kg_words[:].bitcast(FP4X4),
+                    rhs_scale=kg_scales[:],
+                    start=True,
+                    stop=True,
+                )
+                pair.append(bank)
+            scores.append(pair)
+
+        val_pool = []
+        for t in range(PACK):
+            plane = sb.tile([P, T], F32, name="val_pool", tag="staged%d" % t)
+            nc.sync.dma_start(out=plane[:], in_=val_planes[t])
+            val_pool.append(plane)
+
+        w_codes = sb.tile([P, Q], U32, name="w_codes", align_bytes=64)
+        w_scales = sb.tile([P, Q], U8, name="w_scales", align_bytes=64)
+
+        def exponentials(c):
+            b_bank, a_bank = scores[c]
+            col = slice(c, c + 1)
+            b_pages = b_bank[:].rearrange("q (n j) -> q n j", j=PAGE)
+            high = sb.tile([P, PAGES], F32, name="high%d" % c)
+            low = sb.tile([P, PAGES], F32, name="low%d" % c)
+            nc.vector.tensor_reduce(high[:], b_pages, AX.X, ALU.max)
+            nc.vector.tensor_reduce(low[:], b_pages, AX.X, ALU.min)
+            capped = sb.tile([P, PAGES, PAGE], F32, name="capped%d" % c)
+            nc.vector.tensor_tensor(
+                capped[:],
+                a_bank[:].rearrange("q (n j) -> q n j", j=PAGE),
+                high[:].unsqueeze(2).to_broadcast([P, PAGES, PAGE]),
+                ALU.min,
+            )
+            held = sb.tile([P, PAGES, PAGE], F32, name="held%d" % c, align_bytes=64)
+            nc.vector.tensor_tensor(
+                held[:], capped[:], low[:].unsqueeze(2).to_broadcast([P, PAGES, PAGE]), ALU.max
+            )
+            source = held[:].rearrange("q n j -> q (n j)")
+            made = []
+            for k, factor in enumerate((neg_lam, sharp_c)):
+                neg_s = sb.tile([P, I], F32, name="neg_s%d%d" % (c, k), align_bytes=64)
+                neg_max = sb.tile([P, 1], F32, name="neg_max%d%d" % (c, k))
+                nc.vector.tensor_scalar(
+                    neg_s[:], source, factor[:, col], None, ALU.mult, ALU.min, accum_out=neg_max[:]
+                )
+                source = neg_s[:]
+                p = sb.tile([P, PACK, P], F32, name="p", tag=(("turn", "p01"), ("held0", "p11"))[c][k], align_bytes=64)
+                total = sb.tile([P, 1], F32, name="total%d%d" % (c, k))
+                nc.scalar.activation(
+                    p[:].rearrange("q r s -> q s r"),
+                    neg_s[:].rearrange("q (s r) -> q s r", r=PACK),
+                    ACT.Exp,
+                    bias=neg_max[:],
+                    scale=-1.0,
+                    accum_out=total[:],
+                )
+                made.append((p, total))
+            return made
+
+        def turned_weights(c, made, engine):
+            col = slice(c, c + 1)
+            terms = []
+            for k, ((p, total), part) in enumerate(zip(made, (share_c, share_m1))):
+                inverse = sb.tile([P, 1], F32, name="inverse%d%d" % (c, k))
+                nc.vector.reciprocal(inverse[:], total[:])
+                term = sb.tile([P, PACK, P], F32, name="term%d%d" % (c, k))
+                engine.tensor_scalar(term[:], p[:], inverse[:], part[:, col], ALU.mult, ALU.mult)
+                terms.append(term)
+            w_bank = psum.tile([P, PACK, P], F32, name="w_bank%d" % c, tag="bank%d" % c)
+            for k, term in enumerate(terms):
+                for r in range(PACK):
+                    nc.tensor.matmul(
+                        w_bank[:, r, :],
+                        lhsT=term[:, r, :],
+                        rhs=ident[:],
+                        is_transpose=True,
+                        start=(k == 0 and r == 0),
+                        stop=(k == 1 and r == PACK - 1),
+                    )
+            return w_bank
+
+        def quantize_weights(c, w_bank):
+            w_grouped = sb.tile([P, P, PACK], BF16, name="w_grouped%d" % c, align_bytes=64)
+            nc.vector.tensor_tensor(
+                w_grouped[:],
+                w_bank[:].rearrange("s r q -> s q r"),
+                os_c[:].unsqueeze(1).to_broadcast([P, P, PACK]),
+                ALU.mult,
+            )
+            nc.vector.quantize_mx(
+                out=w_codes[:, c * P : (c + 1) * P].bitcast(FP8X4),
+                scales=w_scales[:, c * P : (c + 1) * P],
+                in_=w_grouped[:].rearrange("p w j -> p (w j)"),
+            )
+
+        v_grouped = sb.tile([P, PACK, P, PACK], BF16, name="v_grouped", align_bytes=64)
+        v_codes = sb.tile([P, PACK, P], U32, name="v_codes", align_bytes=64)
+        v_scales = sb.tile([P, PACK, P], U8, name="v_scales", align_bytes=64)
+
+        def values(t, reused):
+            picked = sb.tile([P, I], BF16, name="picked", tag=reused, align_bytes=64)
+            nc.scalar.activation(picked[:], val_pool[t][:].indirect(offsets[:]), ACT.Copy)
+            words = picked[:].bitcast(F32)
+            v_bank = psum.tile([P, 2, P], F32, name="v_bank%d" % t, tag="bank4")
+            for u in range(2):
+                nc.tensor.transpose(v_bank[:, u, :], words[:, u : 2 * P : 2], ident[:])
+            nc.scalar.copy(v_grouped[:, t].bitcast(F32), v_bank[:].rearrange("s u m -> s m u"))
+
+        def quantize_values(t0, t1):
+            nc.vector.quantize_mx(
+                out=v_codes[:, t0:t1, :].rearrange("p t m -> p (t m)").bitcast(FP8X4),
+                scales=v_scales[:, t0:t1, :].rearrange("p t m -> p (t m)"),
+                in_=v_grouped[:, t0:t1].rearrange("p t m r -> p (t m r)"),
+            )
+
+        values(0, "turn")
+        w_bank0 = turned_weights(0, exponentials(0), nc.gpsimd)
+        mem_bank = psum.tile([P, 2, P], F32, name="mem_bank", tag="bank4")
+        for t in range(2):
+            nc.tensor.transpose(mem_bank[:, t, :], mem_c[:, t : t + 1].to_broadcast([P, P]), ident[:])
+        mem_row = sb.tile([P, Q], F32, name="mem_row")
+        nc.scalar.copy(mem_row[:].rearrange("m (p t) -> m p t", t=2), mem_bank[:].rearrange("m t p -> m p t"))
+
+        values(1, "neg_s01")
+        values(2, "held0")
+        made1 = exponentials(1)
+        values(3, "neg_s11")
+        w_bank1 = turned_weights(1, made1, nc.vector)
+        quantize_weights(0, w_bank0)
+        quantize_weights(1, w_bank1)
+        quantize_values(0, 3)
+        quantize_values(3, 4)
+
+        y = sb.tile([P, PACK, Q], F32, name="y")
+        y_grouped = sb.tile([P, Q, PACK], BF16, name="y_grouped", align_bytes=64)
+        out_rows = out_0.rearrange("(p t) q -> p t q", t=PACK)
+
+        def product(t0, t1, q0, q1, tag):
+            o_bank = psum.tile([P, t1 - t0, q1 - q0], F32, name="o_bank", tag=tag)
+            for t in range(t0, t1):
+                nc.tensor.matmul_mx(
+                    out=o_bank[:, t - t0, :],
+                    lhsT=v_codes[:, t, :].bitcast(FP8X4),
+                    lhsT_scale=v_scales[:, t, :],
+                    rhs=w_codes[:, q0:q1].bitcast(FP8X4),
+                    rhs_scale=w_scales[:, q0:q1],
+                    start=True,
+                    stop=True,
+                )
+            return o_bank
+
+        def carry(o_bank, t0, t1, q0, q1):
+            n = min(q1, Q - 1) - q0
+            nc.vector.tensor_tensor(
+                carried[:, t0:t1, q0 + 1 : q0 + 1 + n],
+                o_bank[:, :, 0:n],
+                mem_row[:, q0 + 1 : q0 + 1 + n].unsqueeze(1).to_broadcast([P, t1 - t0, n]),
+                ALU.mult,
+            )
+
+        def change(o_bank, t0, t1, q0, q1):
+            nc.vector.tensor_tensor(y[:, t0:t1, q0:q1], o_bank[:], carried[:, t0:t1, q0:q1], ALU.subtract)
+
+        early = (0, 3, 0, P)
+        late = ((3, 4, 0, Q), (0, 3, P, Q))
+        bank = product(*early, "bank5")
+        carry(bank, *early)
+        change(bank, *early)
+        banks = [product(*part, "bank%d" % (6 + g)) for g, part in enumerate(late)]
+        for bank, part in zip(banks, late):
+            carry(bank, *part)
+        for bank, part in zip(banks, late):
+            change(bank, *part)
+        for c in range(QT):
+            cols = slice(c * P, (c + 1) * P)
+            nc.sync.dma_start(out=out_rows[:, :, cols], in_=y[:, :, cols])
+            dst, src = interleave_views(y_grouped[:, cols, :], y[:, :, cols])
+            if c == 0:
+                nc.scalar.copy(dst, src)
+            else:
+                nc.vector.tensor_copy(dst, src)
+        y_codes = sb.tile([P, Q], U32, name="y_codes", align_bytes=64)
+        y_scales = sb.tile([P, Q], U8, name="y_scales", align_bytes=64)
+        nc.vector.quantize_mx(
+            out=y_codes[:].bitcast(FP8X4), scales=y_scales[:], in_=y_grouped[:].rearrange("p w j -> p (w j)")
+        )
+        nc.sync.dma_start(
+            out=out_1[0].rearrange("p c r -> p (c r)").bitcast(I32), in_=y_codes[:].bitcast(I32)
+        )
+        for quad in range(4):
+            queue = nc.scalar if quad % 2 == 0 else nc.sync
+            queue.dma_start(
+                out=out_2[0, 4 * quad : 4 * quad + 4, :].bitcast(I32),
+                in_=y_scales[32 * quad : 32 * quad + 4, :].bitcast(I32),
+            )

@@ -40,20 +40,20 @@ def tile_attend_pagelimits_twoheats_rowchanges_pl_kernel(
         psum = ctx.enter_context(tc.psum_pool(name="psum", bufs=1))
 
         offsets = sb.tile([P, I // 16], U16, name="offsets")
-        key_words = sb.tile([P, T], U16, name="key_words", tag="staged0")
-        key_scales = sb.tile([P, T], U8, name="key_scales", tag="staged1")
+        key_words = sb.tile([P, T], U16, name="key_words", tag="staged1", align_bytes=64)
+        key_scales = sb.tile([P, T], U8, name="key_scales", tag="staged2", align_bytes=64)
         nc.vector.memset(key_scales[:].bitcast(I32), 0)
         nc.sync.dma_start(offsets[:], offs)
         nc.sync.dma_start(out=key_words[:].bitcast(I32), in_=keys_words[0].bitcast(I32))
         q_raw = [
-            sb.tile([P, PACK, Q], F32, name="limit_query", tag="staged2"),
+            sb.tile([P, PACK, Q], F32, name="limit_query", tag="staged3", align_bytes=64),
         ]
         nc.sync.dma_start(out=q_raw[0][:], in_=query2.rearrange("(p j) q -> p j q", j=PACK))
-        lam_c = sb.tile([P, QT], F32, name="lam_c", tag="staged3")
-        sharp_c = sb.tile([P, QT], F32, name="sharp_c")
+        lam_c = sb.tile([P, QT], F32, name="lam_c", tag="staged4")
+        sharp_c = sb.tile([P, QT], F32, name="sharp_c", tag="staged0", align_bytes=64)
         share_c = sb.tile([P, QT], F32, name="share_c")
         with nc.allow_non_contiguous_dma(reason="one value of each query row to its partition"):
-            for queue, col, src in ((nc.scalar, lam_c, lam), (nc.gpsimd, sharp_c, sharp), (nc.gpsimd, share_c, share)):
+            for queue, col, src in ((nc.scalar, lam_c, lam), (nc.scalar, sharp_c, sharp), (nc.gpsimd, share_c, share)):
                 queue.dma_start(out=col[:], in_=src.rearrange("(c p) o -> p (c o)", p=P))
         for quad in range(4):
             nc.scalar.dma_start(
@@ -68,7 +68,9 @@ def tile_attend_pagelimits_twoheats_rowchanges_pl_kernel(
 
         neg_lam = sb.tile([P, QT], F32, name="neg_lam")
         nc.vector.tensor_scalar(neg_lam[:], lam_c[:], -1.0, None, ALU.mult)
-        q_raw.append(sb.tile([P, PACK, Q], F32, name="score_query", tag="staged3"))
+        neg_heat = sb.tile([P, QT], F32, name="neg_heat")
+        nc.vector.tensor_tensor(neg_heat[:], neg_lam[:], sharp_c[:], ALU.mult)
+        q_raw.append(sb.tile([P, PACK, Q], F32, name="score_query", tag="staged4"))
         nc.sync.dma_start(out=q_raw[1][:], in_=query.rearrange("(p j) q -> p j q", j=PACK))
         ident = sb.tile([P, P], F32, name="ident")
         make_identity(nc, ident[:])
@@ -83,34 +85,32 @@ def tile_attend_pagelimits_twoheats_rowchanges_pl_kernel(
         kg_scales = sb.tile([P, I], U8, name="kg_scales", align_bytes=64)
         nc.vector.tensor_copy(kg_scales[:], key_scales[:].indirect(offsets[:]))
 
-        scores = []
-        for c in range(QT):
-            pair = []
-            for k, raw in enumerate(q_raw):
-                grouped = sb.tile([P, P, PACK], BF16, name="q_grouped", tag=("q_grouped0", "turn")[c], align_bytes=64)
-                dst, src = interleave_views(grouped[:], raw[:, :, c * P : (c + 1) * P])
-                nc.scalar.copy(dst, src)
-                codes = sb.tile([P, P], U32, name="q_codes%d%d" % (c, k), align_bytes=64)
-                scales = sb.tile([P, P], U8, name="q_scales%d%d" % (c, k), align_bytes=64)
-                nc.vector.quantize_mx(
-                    out=codes[:].bitcast(FP8X4), scales=scales[:], in_=grouped[:].rearrange("p w j -> p (w j)")
-                )
-                bank = psum.tile([P, I], F32, name="score%d%d" % (c, k), tag="bank%d" % (2 * c + k))
+        scores = [[], []]
+        for k, raw in enumerate(q_raw):
+            grouped = sb.tile([P, Q, PACK], BF16, name="q_grouped%d" % k, align_bytes=64)
+            dst, src = interleave_views(grouped[:], raw[:])
+            nc.scalar.copy(dst, src)
+            codes = sb.tile([P, Q], U32, name="q_codes%d" % k, align_bytes=64)
+            scales = sb.tile([P, Q], U8, name="q_scales%d" % k, align_bytes=64)
+            nc.vector.quantize_mx(
+                out=codes[:].bitcast(FP8X4), scales=scales[:], in_=grouped[:].rearrange("p w j -> p (w j)")
+            )
+            for c in range(QT):
+                bank = psum.tile([P, I], F32, name="score", tag="bank%d" % (2 * c + k))
                 nc.tensor.matmul_mx(
                     out=bank[:],
-                    lhsT=codes[:].bitcast(FP8X4),
-                    lhsT_scale=scales[:],
+                    lhsT=codes[:, c * P : (c + 1) * P].bitcast(FP8X4),
+                    lhsT_scale=scales[:, c * P : (c + 1) * P],
                     rhs=kg_words[:].bitcast(FP4X4),
                     rhs_scale=kg_scales[:],
                     start=True,
                     stop=True,
                 )
-                pair.append(bank)
-            scores.append(pair)
+                scores[c].append(bank)
 
         val_pool = []
         for t in range(PACK):
-            plane = sb.tile([P, T], F32, name="val_pool", tag="staged%d" % t)
+            plane = sb.tile([P, T], F32, name="val_pool", tag="staged%d" % t, align_bytes=64)
             nc.sync.dma_start(out=plane[:], in_=val_planes[t])
             val_pool.append(plane)
 
@@ -121,31 +121,30 @@ def tile_attend_pagelimits_twoheats_rowchanges_pl_kernel(
             b_bank, a_bank = scores[c]
             col = slice(c, c + 1)
             b_pages = b_bank[:].rearrange("q (n j) -> q n j", j=PAGE)
-            high = sb.tile([P, PAGES], F32, name="high%d" % c)
-            low = sb.tile([P, PAGES], F32, name="low%d" % c)
+            high = sb.tile([P, PAGES], F32, name="high")
+            low = sb.tile([P, PAGES], F32, name="low")
             nc.vector.tensor_reduce(high[:], b_pages, AX.X, ALU.max)
             nc.vector.tensor_reduce(low[:], b_pages, AX.X, ALU.min)
-            capped = sb.tile([P, PAGES, PAGE], F32, name="capped%d" % c)
+            capped = sb.tile([P, PAGES, PAGE], F32, name="capped")
             nc.vector.tensor_tensor(
                 capped[:],
                 a_bank[:].rearrange("q (n j) -> q n j", j=PAGE),
                 high[:].unsqueeze(2).to_broadcast([P, PAGES, PAGE]),
                 ALU.min,
             )
-            held = sb.tile([P, PAGES, PAGE], F32, name="held%d" % c, align_bytes=64)
+            held = sb.tile([P, PAGES, PAGE], F32, name="held")
             nc.vector.tensor_tensor(
                 held[:], capped[:], low[:].unsqueeze(2).to_broadcast([P, PAGES, PAGE]), ALU.max
             )
             source = held[:].rearrange("q n j -> q (n j)")
             made = []
-            for k, factor in enumerate((neg_lam, sharp_c)):
+            for k, factor in enumerate((neg_lam, neg_heat)):
                 neg_s = sb.tile([P, I], F32, name="neg_s%d%d" % (c, k), align_bytes=64)
-                neg_max = sb.tile([P, 1], F32, name="neg_max%d%d" % (c, k))
+                neg_max = sb.tile([P, 1], F32, name="neg_max", tag=("neg_max%d", "total0%d")[c] % k)
                 nc.vector.tensor_scalar(
                     neg_s[:], source, factor[:, col], None, ALU.mult, ALU.min, accum_out=neg_max[:]
                 )
-                source = neg_s[:]
-                p = sb.tile([P, PACK, P], F32, name="p", tag=(("turn", "p01"), ("held0", "p11"))[c][k], align_bytes=64)
+                p = sb.tile([P, PACK, P], F32, name="p", tag=(("staged1", "p01"), ("staged2", "p11"))[c][k], align_bytes=64)
                 total = sb.tile([P, 1], F32, name="total%d%d" % (c, k))
                 nc.scalar.activation(
                     p[:].rearrange("q r s -> q s r"),
@@ -181,7 +180,7 @@ def tile_attend_pagelimits_twoheats_rowchanges_pl_kernel(
             return w_bank
 
         def quantize_weights(c, w_bank):
-            w_grouped = sb.tile([P, P, PACK], BF16, name="w_grouped%d" % c, align_bytes=64)
+            w_grouped = sb.tile([P, P, PACK], BF16, name="w_grouped", tag=("p11", "w_grouped1")[c], align_bytes=64)
             nc.vector.tensor_tensor(
                 w_grouped[:],
                 w_bank[:].rearrange("s r q -> s q r"),
@@ -214,16 +213,16 @@ def tile_attend_pagelimits_twoheats_rowchanges_pl_kernel(
                 in_=v_grouped[:, t0:t1].rearrange("p t m r -> p (t m r)"),
             )
 
-        values(0, "turn")
-        w_bank0 = turned_weights(0, exponentials(0), nc.gpsimd)
+        values(0, "q_grouped1")
         mem_bank = psum.tile([P, 2, P], F32, name="mem_bank", tag="bank4")
         for t in range(2):
             nc.tensor.transpose(mem_bank[:, t, :], mem_c[:, t : t + 1].to_broadcast([P, P]), ident[:])
         mem_row = sb.tile([P, Q], F32, name="mem_row")
         nc.scalar.copy(mem_row[:].rearrange("m (p t) -> m p t", t=2), mem_bank[:].rearrange("m t p -> m p t"))
 
-        values(1, "neg_s01")
-        values(2, "held0")
+        values(1, "picked1")
+        w_bank0 = turned_weights(0, exponentials(0), nc.gpsimd)
+        values(2, "neg_s01")
         made1 = exponentials(1)
         values(3, "neg_s11")
         w_bank1 = turned_weights(1, made1, nc.vector)

@@ -82,31 +82,48 @@ def tile_attend_pagelimits_twoheats_rowchanges_pl_kernel(
 
         kg_words = sb.tile([P, I], U16, name="kg_words", align_bytes=64)
         nc.vector.tensor_copy(kg_words[:], key_words[:].indirect(offsets[:]))
-        kg_scales = sb.tile([P, I], U8, name="kg_scales", align_bytes=64)
-        nc.vector.tensor_copy(kg_scales[:], key_scales[:].indirect(offsets[:]))
+        half = I // 2
+        kg_scales = []
 
-        scores = [[], []]
-        for k, raw in enumerate(q_raw):
-            grouped = sb.tile([P, Q, PACK], BF16, name="q_grouped%d" % k, align_bytes=64)
-            dst, src = interleave_views(grouped[:], raw[:])
+        def gather_scales(h, tag):
+            picked = sb.tile([P, half], U8, name="kg_scales", tag=tag, align_bytes=64)
+            columns = half // 16
+            nc.vector.tensor_copy(picked[:], key_scales[:].indirect(offsets[:, h * columns : (h + 1) * columns]))
+            kg_scales.append(picked)
+
+        def quantize_query(c, k):
+            grouped = sb.tile([P, P, PACK], BF16, name="q_grouped%d%d" % (c, k), align_bytes=64)
+            dst, src = interleave_views(grouped[:], q_raw[k][:, :, c * P : (c + 1) * P])
             nc.scalar.copy(dst, src)
-            codes = sb.tile([P, Q], U32, name="q_codes%d" % k, align_bytes=64)
-            scales = sb.tile([P, Q], U8, name="q_scales%d" % k, align_bytes=64)
+            codes = sb.tile([P, P], U32, name="q_codes%d%d" % (c, k), align_bytes=64)
+            scales = sb.tile([P, P], U8, name="q_scales%d%d" % (c, k), align_bytes=64)
             nc.vector.quantize_mx(
                 out=codes[:].bitcast(FP8X4), scales=scales[:], in_=grouped[:].rearrange("p w j -> p (w j)")
             )
-            for c in range(QT):
+            return codes, scales
+
+        gather_scales(0, "kg_scales0")
+        first = quantize_query(0, 0)
+        gather_scales(1, "q_grouped00")
+
+        scores = []
+        for c in range(QT):
+            pair = []
+            for k in range(2):
+                codes, scales = first if (c, k) == (0, 0) else quantize_query(c, k)
                 bank = psum.tile([P, I], F32, name="score", tag="bank%d" % (2 * c + k))
-                nc.tensor.matmul_mx(
-                    out=bank[:],
-                    lhsT=codes[:, c * P : (c + 1) * P].bitcast(FP8X4),
-                    lhsT_scale=scales[:, c * P : (c + 1) * P],
-                    rhs=kg_words[:].bitcast(FP4X4),
-                    rhs_scale=kg_scales[:],
-                    start=True,
-                    stop=True,
-                )
-                scores[c].append(bank)
+                for h in range(2):
+                    nc.tensor.matmul_mx(
+                        out=bank[:, h * half : (h + 1) * half],
+                        lhsT=codes[:].bitcast(FP8X4),
+                        lhsT_scale=scales[:],
+                        rhs=kg_words[:, h * half : (h + 1) * half].bitcast(FP4X4),
+                        rhs_scale=kg_scales[h][:],
+                        start=True,
+                        stop=True,
+                    )
+                pair.append(bank)
+            scores.append(pair)
 
         val_pool = []
         for t in range(PACK):
@@ -157,14 +174,14 @@ def tile_attend_pagelimits_twoheats_rowchanges_pl_kernel(
                 made.append((p, total))
             return made
 
-        def turned_weights(c, made, engine):
+        def turned_weights(c, made):
             col = slice(c, c + 1)
             terms = []
             for k, ((p, total), part) in enumerate(zip(made, (share_c, share_m1))):
                 inverse = sb.tile([P, 1], F32, name="inverse%d%d" % (c, k))
                 nc.vector.reciprocal(inverse[:], total[:])
                 term = sb.tile([P, PACK, P], F32, name="term%d%d" % (c, k))
-                engine.tensor_scalar(term[:], p[:], inverse[:], part[:, col], ALU.mult, ALU.mult)
+                nc.vector.tensor_scalar(term[:], p[:], inverse[:], part[:, col], ALU.mult, ALU.mult)
                 terms.append(term)
             w_bank = psum.tile([P, PACK, P], F32, name="w_bank%d" % c, tag="bank%d" % c)
             for k, term in enumerate(terms):
@@ -213,7 +230,7 @@ def tile_attend_pagelimits_twoheats_rowchanges_pl_kernel(
                 in_=v_grouped[:, t0:t1].rearrange("p t m r -> p (t m r)"),
             )
 
-        values(0, "q_grouped1")
+        values(0, "q_grouped11")
         mem_bank = psum.tile([P, 2, P], F32, name="mem_bank", tag="bank4")
         for t in range(2):
             nc.tensor.transpose(mem_bank[:, t, :], mem_c[:, t : t + 1].to_broadcast([P, P]), ident[:])
@@ -221,11 +238,11 @@ def tile_attend_pagelimits_twoheats_rowchanges_pl_kernel(
         nc.scalar.copy(mem_row[:].rearrange("m (p t) -> m p t", t=2), mem_bank[:].rearrange("m t p -> m p t"))
 
         values(1, "picked1")
-        w_bank0 = turned_weights(0, exponentials(0), nc.gpsimd)
+        w_bank0 = turned_weights(0, exponentials(0))
         values(2, "neg_s01")
         made1 = exponentials(1)
         values(3, "neg_s11")
-        w_bank1 = turned_weights(1, made1, nc.vector)
+        w_bank1 = turned_weights(1, made1)
         quantize_weights(0, w_bank0)
         quantize_weights(1, w_bank1)
         quantize_values(0, 3)
@@ -263,7 +280,7 @@ def tile_attend_pagelimits_twoheats_rowchanges_pl_kernel(
 
         early = (0, 3, 0, P)
         late = ((3, 4, 0, Q), (0, 3, P, Q))
-        bank = product(*early, "bank5")
+        bank = product(*early, "bank4")
         carry(bank, *early)
         change(bank, *early)
         banks = [product(*part, "bank%d" % (6 + g)) for g, part in enumerate(late)]

from contextlib import ExitStack

import concourse.mybir as mybir
from concourse.masks import make_identity

D, T, I, Q, E, PAGE = 512, 2048, 512, 256, 512, 8
FLOPS = 2 * (2 * D * Q * I + I * E * Q)

F32 = mybir.dt.float32
BF16 = mybir.dt.bfloat16
I32 = mybir.dt.int32
U32 = mybir.dt.uint32
U16 = mybir.dt.uint16
U8 = mybir.dt.uint8
FP8X4 = mybir.dt.float8_e4m3fn_x4
FP4X4 = mybir.dt.float4_e2m1fn_x4
ALU = mybir.AluOpType
ACT = mybir.ActivationFunctionType
AX = mybir.AxisListType

P = 128
PACK = 4
QT = Q // P
PAGES = I // PAGE


def interleave_views(grouped, planes):
    return (
        grouped.rearrange("p (c i) t -> p c t i", i=4),
        planes.rearrange("p t (c i) -> p c t i", i=4),
    )


def tile_attend_pagelimits_twoheats_rowchanges_pl_kernel(
    tc, query, query2, keys_words, keys_scales, lam, sharp, share, slot_factor, vals, memq, offs, out_0, out_1, out_2
):
    nc = tc.nc
    with ExitStack() as ctx:
        sb = ctx.enter_context(tc.tile_pool(name="sb", bufs=1))
        psum = ctx.enter_context(tc.psum_pool(name="psum", bufs=1))

        offsets = sb.tile([P, I // 16], U16, name="offsets")
        key_words = sb.tile([P, T], U16, name="key_words", tag="staged1", align_bytes=64)
        key_scales = sb.tile([P, T], U8, name="key_scales", tag="staged2", align_bytes=64)
        nc.vector.memset(key_scales[:].bitcast(I32), 0)
        nc.sync.dma_start(offsets[:], offs)
        nc.sync.dma_start(out=key_words[:].bitcast(I32), in_=keys_words[0].bitcast(I32))
        q_raw = [
            sb.tile([P, PACK, Q], F32, name="limit_query", tag="staged3", align_bytes=64),
        ]
        nc.sync.dma_start(out=q_raw[0][:], in_=query2.rearrange("(p j) q -> p j q", j=PACK))
        lam_c = sb.tile([P, QT], F32, name="lam_c", tag="staged4")
        sharp_c = sb.tile([P, QT], F32, name="sharp_c", tag="staged0", align_bytes=64)
        share_c = sb.tile([P, QT], F32, name="share_c")
        with nc.allow_non_contiguous_dma(reason="one value of each query row to its partition"):
            for queue, col, src in ((nc.scalar, lam_c, lam), (nc.scalar, sharp_c, sharp), (nc.gpsimd, share_c, share)):
                queue.dma_start(out=col[:], in_=src.rearrange("(c p) o -> p (c o)", p=P))
        for quad in range(4):
            nc.scalar.dma_start(
                out=key_scales[32 * quad : 32 * quad + 4, :].bitcast(I32),
                in_=keys_scales[0, 4 * quad : 4 * quad + 4, :].bitcast(I32),
            )
        os_c = sb.tile([P, PACK], F32, name="os_c")
        nc.gpsimd.dma_start(out=os_c[:], in_=slot_factor.rearrange("o (s r) -> (o s) r", r=PACK))
        mem_c = sb.tile([P, 2], F32, name="mem_c")
        nc.gpsimd.dma_start(out=mem_c[:], in_=memq.rearrange("o (p t) -> (o p) t", t=2))
        val_planes = vals.rearrange("(p t) n -> t p n", t=PACK)

        neg_lam = sb.tile([P, QT], F32, name="neg_lam")
        nc.vector.tensor_scalar(neg_lam[:], lam_c[:], -1.0, None, ALU.mult)
        neg_heat = sb.tile([P, QT], F32, name="neg_heat")
        nc.vector.tensor_tensor(neg_heat[:], neg_lam[:], sharp_c[:], ALU.mult)
        q_raw.append(sb.tile([P, PACK, Q], F32, name="score_query", tag="staged4"))
        nc.sync.dma_start(out=q_raw[1][:], in_=query.rearrange("(p j) q -> p j q", j=PACK))
        ident = sb.tile([P, P], F32, name="ident")
        make_identity(nc, ident[:])
        share_m1 = sb.tile([P, QT], F32, name="share_m1")
        nc.gpsimd.tensor_scalar(share_m1[:], share_c[:], 1.0, -1.0, ALU.mult, ALU.add)

        carried = sb.tile([P, PACK, Q], F32, name="carried")
        nc.vector.memset(carried[:, :, 0:1], 0.0)

        kg_words = sb.tile([P, I], U16, name="kg_words", align_bytes=64)
        nc.vector.tensor_copy(kg_words[:], key_words[:].indirect(offsets[:]))
        half = I // 2
        kg_scales = []

        def gather_scales(h, tag):
            picked = sb.tile([P, half], U8, name="kg_scales", tag=tag, align_bytes=64)
            columns = half // 16
            nc.vector.tensor_copy(picked[:], key_scales[:].indirect(offsets[:, h * columns : (h + 1) * columns]))
            kg_scales.append(picked)

        def quantize_query(c, k):
            grouped = sb.tile([P, P, PACK], BF16, name="q_grouped%d%d" % (c, k), align_bytes=64)
            dst, src = interleave_views(grouped[:], q_raw[k][:, :, c * P : (c + 1) * P])
            nc.scalar.copy(dst, src)
            codes = sb.tile([P, P], U32, name="q_codes%d%d" % (c, k), align_bytes=64)
            scales = sb.tile([P, P], U8, name="q_scales%d%d" % (c, k), align_bytes=64)
            nc.vector.quantize_mx(
                out=codes[:].bitcast(FP8X4), scales=scales[:], in_=grouped[:].rearrange("p w j -> p (w j)")
            )
            return codes, scales

        gather_scales(0, "kg_scales0")
        first = quantize_query(0, 0)
        gather_scales(1, "q_grouped00")

        scores = []
        for c in range(QT):
            pair = []
            for k in range(2):
                codes, scales = first if (c, k) == (0, 0) else quantize_query(c, k)
                bank = psum.tile([P, I], F32, name="score", tag="bank%d" % (2 * c + k))
                for h in range(2):
                    nc.tensor.matmul_mx(
                        out=bank[:, h * half : (h + 1) * half],
                        lhsT=codes[:].bitcast(FP8X4),
                        lhsT_scale=scales[:],
                        rhs=kg_words[:, h * half : (h + 1) * half].bitcast(FP4X4),
                        rhs_scale=kg_scales[h][:],
                        start=True,
                        stop=True,
                    )
                pair.append(bank)
            scores.append(pair)

        val_pool = []
        for t in range(PACK):
            plane = sb.tile([P, T], F32, name="val_pool", tag="staged%d" % t, align_bytes=64)
            nc.sync.dma_start(out=plane[:], in_=val_planes[t])
            val_pool.append(plane)

        w_codes = sb.tile([P, Q], U32, name="w_codes", align_bytes=64)
        w_scales = sb.tile([P, Q], U8, name="w_scales", align_bytes=64)

        def exponentials(c):
            b_bank, a_bank = scores[c]
            col = slice(c, c + 1)
            b_pages = b_bank[:].rearrange("q (n j) -> q n j", j=PAGE)
            high = sb.tile([P, PAGES], F32, name="high")
            low = sb.tile([P, PAGES], F32, name="low")
            nc.vector.tensor_reduce(high[:], b_pages, AX.X, ALU.max)
            nc.vector.tensor_reduce(low[:], b_pages, AX.X, ALU.min)
            capped = sb.tile([P, PAGES, PAGE], F32, name="capped")
            nc.vector.tensor_tensor(
                capped[:],
                a_bank[:].rearrange("q (n j) -> q n j", j=PAGE),
                high[:].unsqueeze(2).to_broadcast([P, PAGES, PAGE]),
                ALU.min,
            )
            held = sb.tile([P, PAGES, PAGE], F32, name="held")
            nc.vector.tensor_tensor(
                held[:], capped[:], low[:].unsqueeze(2).to_broadcast([P, PAGES, PAGE]), ALU.max
            )
            source = held[:].rearrange("q n j -> q (n j)")
            made = []
            for k, factor in enumerate((neg_lam, neg_heat)):
                neg_s = sb.tile([P, I], F32, name="neg_s%d%d" % (c, k), align_bytes=64)
                neg_max = sb.tile([P, 1], F32, name="neg_max", tag=("neg_max%d", "total0%d")[c] % k)
                nc.vector.tensor_scalar(
                    neg_s[:], source, factor[:, col], None, ALU.mult, ALU.min, accum_out=neg_max[:]
                )
                p = sb.tile([P, PACK, P], F32, name="p", tag=(("staged1", "p01"), ("staged2", "p11"))[c][k], align_bytes=64)
                total = sb.tile([P, 1], F32, name="total%d%d" % (c, k))
                nc.scalar.activation(
                    p[:].rearrange("q r s -> q s r"),
                    neg_s[:].rearrange("q (s r) -> q s r", r=PACK),
                    ACT.Exp,
                    bias=neg_max[:],
                    scale=-1.0,
                    accum_out=total[:],
                )
                made.append((p, total))
            return made

        def turned_weights(c, made):
            col = slice(c, c + 1)
            terms = []
            for k, ((p, total), part) in enumerate(zip(made, (share_c, share_m1))):
                inverse = sb.tile([P, 1], F32, name="inverse%d%d" % (c, k))
                nc.vector.reciprocal(inverse[:], total[:])
                term = sb.tile([P, PACK, P], F32, name="term%d%d" % (c, k))
                nc.vector.tensor_scalar(term[:], p[:], inverse[:], part[:, col], ALU.mult, ALU.mult)
                terms.append(term)
            w_bank = psum.tile([P, PACK, P], F32, name="w_bank%d" % c, tag="bank%d" % c)
            for k, term in enumerate(terms):
                for r in range(PACK):
                    nc.tensor.matmul(
                        w_bank[:, r, :],
                        lhsT=term[:, r, :],
                        rhs=ident[:],
                        is_transpose=True,
                        start=(k == 0 and r == 0),
                        stop=(k == 1 and r == PACK - 1),
                    )
            return w_bank

        def quantize_weights(c, w_bank):
            w_grouped = sb.tile([P, P, PACK], BF16, name="w_grouped", tag=("p11", "w_grouped1")[c], align_bytes=64)
            nc.vector.tensor_tensor(
                w_grouped[:],
                w_bank[:].rearrange("s r q -> s q r"),
                os_c[:].unsqueeze(1).to_broadcast([P, P, PACK]),
                ALU.mult,
            )
            nc.vector.quantize_mx(
                out=w_codes[:, c * P : (c + 1) * P].bitcast(FP8X4),
                scales=w_scales[:, c * P : (c + 1) * P],
                in_=w_grouped[:].rearrange("p w j -> p (w j)"),
            )

        v_grouped = sb.tile([P, PACK, P, PACK], BF16, name="v_grouped", align_bytes=64)
        v_codes = sb.tile([P, PACK, P], U32, name="v_codes", align_bytes=64)
        v_scales = sb.tile([P, PACK, P], U8, name="v_scales", align_bytes=64)

        def values(t, reused):
            picked = sb.tile([P, I], BF16, name="picked", tag=reused, align_bytes=64)
            nc.scalar.activation(picked[:], val_pool[t][:].indirect(offsets[:]), ACT.Copy)
            words = picked[:].bitcast(F32)
            v_bank = psum.tile([P, 2, P], F32, name="v_bank%d" % t, tag="bank4")
            for u in range(2):
                nc.tensor.transpose(v_bank[:, u, :], words[:, u : 2 * P : 2], ident[:])
            nc.scalar.copy(v_grouped[:, t].bitcast(F32), v_bank[:].rearrange("s u m -> s m u"))

        def quantize_values(t0, t1):
            nc.vector.quantize_mx(
                out=v_codes[:, t0:t1, :].rearrange("p t m -> p (t m)").bitcast(FP8X4),
                scales=v_scales[:, t0:t1, :].rearrange("p t m -> p (t m)"),
                in_=v_grouped[:, t0:t1].rearrange("p t m r -> p (t m r)"),
            )

        values(0, "q_grouped11")
        mem_bank = psum.tile([P, 2, P], F32, name="mem_bank", tag="bank4")
        for t in range(2):
            nc.tensor.transpose(mem_bank[:, t, :], mem_c[:, t : t + 1].to_broadcast([P, P]), ident[:])
        mem_row = sb.tile([P, Q], F32, name="mem_row")
        nc.scalar.copy(mem_row[:].rearrange("m (p t) -> m p t", t=2), mem_bank[:].rearrange("m t p -> m p t"))

        values(1, "picked1")
        w_bank0 = turned_weights(0, exponentials(0))
        values(2, "neg_s01")
        made1 = exponentials(1)
        values(3, "neg_s11")
        w_bank1 = turned_weights(1, made1)
        quantize_weights(0, w_bank0)
        quantize_weights(1, w_bank1)
        quantize_values(0, 3)
        quantize_values(3, 4)

        y = sb.tile([P, PACK, Q], F32, name="y")
        y_grouped = sb.tile([P, Q, PACK], BF16, name="y_grouped", align_bytes=64)
        out_rows = out_0.rearrange("(p t) q -> p t q", t=PACK)

        def product(t0, t1, q0, q1, tag):
            o_bank = psum.tile([P, t1 - t0, q1 - q0], F32, name="o_bank", tag=tag)
            for t in range(t0, t1):
                nc.tensor.matmul_mx(
                    out=o_bank[:, t - t0, :],
                    lhsT=v_codes[:, t, :].bitcast(FP8X4),
                    lhsT_scale=v_scales[:, t, :],
                    rhs=w_codes[:, q0:q1].bitcast(FP8X4),
                    rhs_scale=w_scales[:, q0:q1],
                    start=True,
                    stop=True,
                )
            return o_bank

        def carry(o_bank, t0, t1, q0, q1):
            n = min(q1, Q - 1) - q0
            nc.vector.tensor_tensor(
                carried[:, t0:t1, q0 + 1 : q0 + 1 + n],
                o_bank[:, :, 0:n],
                mem_row[:, q0 + 1 : q0 + 1 + n].unsqueeze(1).to_broadcast([P, t1 - t0, n]),
                ALU.mult,
            )

        def change(o_bank, t0, t1, q0, q1):
            nc.vector.tensor_tensor(y[:, t0:t1, q0:q1], o_bank[:], carried[:, t0:t1, q0:q1], ALU.subtract)

        early = (0, 3, 0, P)
        late = ((3, 4, 0, Q), (0, 3, P, Q))
        bank = product(*early, "bank4")
        carry(bank, *early)
        change(bank, *early)
        banks = [product(*part, "bank%d" % (6 + g)) for g, part in enumerate(late)]
        for bank, part in zip(banks, late):
            carry(bank, *part)
        for bank, part in zip(banks, late):
            change(bank, *part)
        for c in range(QT):
            cols = slice(c * P, (c + 1) * P)
            nc.sync.dma_start(out=out_rows[:, :, cols], in_=y[:, :, cols])
            dst, src = interleave_views(y_grouped[:, cols, :], y[:, :, cols])
            if c == 0:
                nc.scalar.copy(dst, src)
            else:
                nc.vector.tensor_copy(dst, src)
        y_codes = sb.tile([P, Q], U32, name="y_codes", align_bytes=64)
        y_scales = sb.tile([P, Q], U8, name="y_scales", align_bytes=64)
        nc.vector.quantize_mx(
            out=y_codes[:].bitcast(FP8X4), scales=y_scales[:], in_=y_grouped[:].rearrange("p w j -> p (w j)")
        )
        nc.sync.dma_start(
            out=out_1[0].rearrange("p c r -> p (c r)").bitcast(I32), in_=y_codes[:].bitcast(I32)
        )
        for quad in range(4):
            queue = nc.scalar if quad % 2 == 0 else nc.sync
            queue.dma_start(
                out=out_2[0, 4 * quad : 4 * quad + 4, :].bitcast(I32),
                in_=y_scales[32 * quad : 32 * quad + 4, :].bitcast(I32),
            )
